import numpy as np, ml_dtypes
CORES = [9,25,41,57]
N = 4
BF = ml_dtypes.bfloat16
def gentries(a):
    return np.ascontiguousarray(a.reshape(8, 16, -1).transpose(0, 2, 1)).reshape(8, -1)
def gtable(e):
    e = np.asarray(e); return np.ascontiguousarray(e.reshape(8, -1, 16).transpose(0, 2, 1)).reshape(128, -1).astype(np.int32)
W, S, J, RO, LW = 4096, 16, 256, 12, 12
K = S * J
def pack(x, p, c):
    return {"ring": np.ascontiguousarray(x.reshape(N, 128, W)).astype(np.float32).astype(BF), "place": np.stack([gtable(a.reshape(8, K)) for a in p]),
            "carry": np.ascontiguousarray(c.reshape(N, 128, J)).astype(np.float32).astype(BF)}
def parts(rng):
    return rng.integers(0, 16, (N, 8, 16, W)), rng.integers(0, W, (N, 8, J, S)), rng.integers(0, 16, (N, 8, 16, J))
def extremes(rng, n):
    m = rng.integers(0, 4, (N, 8, 1, n))
    return np.where(m == 0, 0, np.where(m == 1, 15, 15 * rng.integers(0, 2, (N, 8, 16, n))))
def single(rng, hit):
    dig = rng.integers(0, 16, hit.shape)
    return (hit & (np.arange(16)[:, None] == dig)).astype(np.int64)
def setup_inputs(rng):
    x, p, c = parts(rng)
    return pack(x, p, c)
def setup_inputs_spread(rng):
    top = rng.choice(np.array([0, 1, 3, 7, 15]), (N, 8, 1, W)); x = ((top + 1) * rng.random((N, 8, 16, W))).astype(np.int64)
    top = rng.choice(np.array([0, 1, 3, 7, 15]), (N, 8, 1, J)); c = ((top + 1) * rng.random((N, 8, 16, J))).astype(np.int64)
    wd = 2 ** rng.integers(0, LW + 1, (N, 8, J, 1))
    p = (rng.integers(0, W, (N, 8, J, 1)) + (wd * rng.random((N, 8, J, S))).astype(np.int64)) & (W - 1)
    x[..., 5::16] = 15; x[..., 6::16] = 0; x[..., 7::16] = 8; h = 16 * rng.integers(0, W // 16, (N, 8, J, S))
    for j, a in ((0, 15), (2, 14), (J - 3, 14), (J - 1, 15)):
        c[:, :, :, j] = a; p[:, :, j] = h[:, :, j] + 5
    for j in (1, J - 2):
        c[:, :, :, j] = 0; p[:, :, j] = h[:, :, j] + 6; p[:, :, j, 0] += 1; p[:, :, j, S - 1] += 1
    return pack(x, p, c)
def setup_inputs_ends(rng):
    x = extremes(rng, W); c = extremes(rng, J); m = rng.integers(0, 4, (N, 8, J, 1))
    p = (W - 1) * np.where(m == 0, 0, np.where(m == 1, 1, rng.integers(0, 2, (N, 8, J, S))))
    x[:, 1::2, :, W - 1] = 15; x[:, 1::2, :, 0] = 0; x[:, 0::4, :, W - 1] = 0; x[:, 0::4, :, 0] = 15
    for j in (0, 3, J - 1):
        c[:, :, :, j] = 15; p[:, 1::2, j] = W - 1; p[:, 0::4, j] = 0
    for j in (1, 4, J - 2):
        c[:, :, :, j] = 0; p[:, 1::2, j] = 0; p[:, 0::4, j] = W - 1
    return pack(x, p, c)
def setup_inputs_corners(rng):
    x, p, c = parts(rng); run = np.arange(K).reshape(J, S) & (W - 1)
    for q in range(N):
        for g, m in enumerate(rng.permutation(8)):
            a = int(rng.integers(0, W))
            if m == 0: p[q, g] = a
            elif m == 1: p[q, g] = W - 1; c[q, g] = 15
            elif m == 2: p[q, g] = 0; c[q, g] = 0
            elif m == 3:
                p[q, g] = a; p[q, g, rng.integers(0, J), rng.integers(0, S)] = (a + 1 + rng.integers(0, W - 1)) & (W - 1)
            elif m == 4: p[q, g] = run
            elif m == 5: p[q, g] = W - 1 - run
            elif m == 6:
                x[q, g] = 0; x[q, g, :, W - 1] = 15; p[q, g] = rng.integers(-4, 4, (J, S)) & (W - 1)
            else:
                x[q, g] = 15; c[q, g, :, J - 1] = 15; c[q, g, :, J - 2] = 0
                s = np.add.reduce(c[q, g], axis=0); p[q, g, :, 0] = (W - s - (np.arange(J) & 1)) & (W - 1)
    return pack(x, p, c)
def setup_inputs_calm(rng):
    hit = rng.random((N, 8, 1, W)) < rng.choice(np.array([0.002, 0.008, 0.02]), (N, 8, 1, 1)); hit[..., :32] = False; hit[..., W - 8:] = False
    x = single(rng, hit); c = single(rng, rng.random((N, 8, 1, J)) < 0.25) * rng.integers(1, 4, (N, 8, 1, J))
    p = np.where(rng.random((N, 8, J, S)) < 0.5, rng.integers(-4, 4, (N, 8, J, S)) & (W - 1), rng.integers(0, W, (N, 8, J, S)))
    q = int(rng.integers(0, N)); g = int(rng.integers(0, 8)); c[q, g] = 0
    for t in range(RO):
        x[q, g] = 0; q = (q + 1 + t % (N - 1)) % N; g = (g + 1) % 8
    return pack(x, p, c)
def setup_inputs_full(rng):
    hit = rng.random((N, 8, 1, W)) < 0.004; top = 14 if S == 8 else 15
    for b in (0, 1): hit[..., (W - 1 - b + 240 * np.arange(-RO, RO + 1)) & (W - 1)] = False
    hit[:, 1::2, :, 15::16] = False
    x = single(rng, hit); x[:, 0::2] = 15 * x[:, 0::2]; x[:, 1::2] = top - x[:, 1::2]
    c = 15 - single(rng, rng.random((N, 8, 1, J)) < 0.125)
    late = (W - 1 - rng.integers(0, 2, (N, 8, J, S)) - 240 * rng.integers(0, RO, (N, 8, J, S))) & (W - 1)
    p = np.where(rng.random((N, 8, J, S)) < 0.5, late, rng.integers(0, W, (N, 8, J, S)))
    e = (W - 1 + 240 * (RO - 1)) & (W - 1); x[:, 0::2, :, e] = 7; x[:, 1::2, :, e] = 3
    c[:, :, :, J - 1] = 15; p[:, 1::2, J - 1] = W - 1; p[:, 0::2, J - 1] = late[:, 0::2, J - 1]; p[:, 0::2, J - 1, 0] = W - 1; p[:, 0::2, J - 1, S - 1] = W - 1
    return pack(x, p, c)
def check_inputs(d):
    bad = []
    for k, lo, hi in (("ring", 0, 15), ("place", 0, W - 1), ("carry", 0, 15)):
        a = np.asarray(d[k]).astype(np.float64)
        if not (np.min(a) >= lo and np.max(a) <= hi): bad.append("range of " + k)
        if np.any(a != np.floor(a)): bad.append("whole numbers in " + k)
    return bad
def reference(ring, place, carry):
    x = ring.astype(np.float32).astype(np.int32).reshape(N, 8, 16, W); c = carry.astype(np.float32).astype(np.int32).reshape(N, 8, 16, J)
    p = np.stack([gentries(a) for a in place]).astype(np.int64); shown = []
    for t in range(RO):
        v = np.take_along_axis(x, p[:, :, None, :], 3).reshape(N, 8, 16, J, S)
        after = (c[..., None] + np.add.accumulate(v, axis=4, dtype=np.int32)) & 15
        into = np.concatenate([c[..., None], after[..., :S - 1]], axis=4)
        p = (p + np.add.reduce(into, axis=2).reshape(N, 8, K)) & (W - 1)
        end = np.ascontiguousarray(after[..., S - 1]); shown.append(end.reshape(N, 128, J))
        c = np.roll(end, (1 + t % (N - 1), 1), axis=(0, 1))
    return {"yp": np.stack([gtable(a) for a in p]).astype(np.float32), "yc": np.concatenate(shown, axis=2).astype(np.float32).astype(BF)}

@@ -1,0 +1,280 @@
+from concourse.mybir import AluOpType as A, ActivationFunctionType as F
+
+W, S, J, RO = 4096, 16, 256, 12
+GROW = 15 * 16
+B = 3072.0
+NS = [64, 64, 64, 64]
+VS = [18, 18, 18, 18]
+V0 = [32, 18, 18, 18]
+C = len(NS)
+NM = max(NS)
+LO = [sum(NS[:c]) for c in range(C)]
+EXT = [(1, 3), (4, 7), (8, 11)]
+YB = [(0, 3), (4, 7), (8, 10)]
+PAT_V = [("scan", 0), ("add", -1), ("gV", 2), ("conv", -1), ("ins", 1), ("ev", 0)]
+PAT_S = [("q16", 0), ("gS", 2)]
+PAT_P = [("pc", 0), ("p15", 1), ("pin", 1), ("pq", 0), ("px", 1)]
+PAT_G = [("rem", 0), ("z", 2)]
+
+SCRATCH = {
+    "win": ("sbuf", [128, W + GROW * (RO - 1)], "bfloat16"),
+    "xb": ("sbuf", [128, J * S], "bfloat16"),
+    "qb": ("sbuf", [128, J * S], "bfloat16"),
+    "base": ("sbuf", [128, NM * S], "bfloat16"),
+    "land": ("sbuf", [128, RO * J], "bfloat16"),
+    "cb": ("sbuf", [128, RO * J], "bfloat16"),
+    "q16": ("sbuf", [128, J], "bfloat16"),
+    "off": ("sbuf", [128, J], "uint16"),
+    "plc": ("sbuf", [128, J], "int32"),
+    "plf": ("sbuf", [128, J], "float32"),
+    "msk": ("sbuf", [128, J], "float32"),
+    "ypo": ("sbuf", [128, J], "float32"),
+    "pi": ("sbuf", [128, 8], "int32"),
+    "col": ("sbuf", [128, 8], "float32"),
+    "uu": ("sbuf", [128, 2 * RO], "float32"),
+    "kc": ("sbuf", [128, 2 * RO], "float32"),
+    "ee": ("sbuf", [128, 144], "bfloat16"),
+    "dd": ("sbuf", [128, 144], "bfloat16"),
+    "d1": ("sbuf", [128, 128], "bfloat16"),
+    "d2": ("sbuf", [128, 128], "bfloat16"),
+    "ab": ("sbuf", [128, 128], "bfloat16"),
+    "ad": ("sbuf", [128, 128], "bfloat16"),
+    "qw": ("sbuf", [128, 144], "bfloat16"),
+    "xsel": ("sbuf", [128, S * 128], "bfloat16"),
+    "shp": ("sbuf", [128, 128], "bfloat16"),
+    "sh0": ("sbuf", [128, 128], "bfloat16"),
+    "idp": ("sbuf", [128, 128], "bfloat16"),
+    "idf": ("sbuf", [128, 128], "float32"),
+    "one": ("sbuf", [128, NM], "bfloat16"),
+    "cw": ("sbuf", [128, 128], "bfloat16"),
+    "ci": ("sbuf", [128, 128], "bfloat16"),
+}
+for _c in range(C):
+    SCRATCH["pc%d" % _c] = ("psum", [128, 512], "float32")
+for _c in range(2):
+    SCRATCH["acc%d" % _c] = ("psum", [128, 512], "float32")
+    SCRATCH["pin%d" % _c] = ("psum", [128, 512], "float32")
+
+SEMAPHORES = (["cV", "cS", "cP", "cG", "ring", "place", "carry", "sent", "out"]
+              + ["ext%d" % i for i in range(len(EXT))]
+              + ["arr%d_%d" % (c, t) for c in range(C) for t in range(RO - 1)])
+
+
+def periodic(pat, ops):
+    seq = []
+    for m in range(-C, (RO + 1) * C):
+        for k, d in pat:
+            x = m + d
+            if 0 <= x < RO * C and (k, x % C, x // C) in ops:
+                seq.append((k, x % C, x // C))
+    return seq
+
+
+def rank_program(g, core, T, topo):
+    rank = T.rank_of(core)
+    if rank is None:
+        return
+    N = len(T.cores)
+    V, Sc, P, Y = g.vector, g.scalar, g.tensor, g.sync
+    queue = {"V": V, "S": Sc, "P": P, "G": g, "Y": Y}
+    ops = {}
+
+    def op(name, q, deps, fn, sem=None, inc=1):
+        ops[name] = (q, list(deps), fn, sem or "c" + q, inc)
+
+    small = dict(allow_small_or_imprecise_dtypes=True)
+
+    op("ring", "Y", [], lambda: Y.dma_start(T.win[:, 0:W], T.ring[:, :]), "ring", 16)
+    op("place", "S", [], lambda: Sc.dma_start(T.plc[:, :], T.place[:, :]), "place", 16)
+    op("carry", "Y", [], lambda: Y.dma_start(T.land[:, 0:J], T.carry[:, :]), "carry", 16)
+
+    def ext(i):
+        a, b = GROW * (EXT[i][0] - 1), GROW * EXT[i][1]
+        return lambda: Y.dma_start(T.win[:, W + a:W + b], T.ring[:, a:b])
+    for i in range(len(EXT)):
+        op(("ext", i), "Y", ["ring"] if i == 0 else [("ev", C - 1, EXT[i][0] - 3)], ext(i), "ext%d" % i, 16)
+
+    op("pi", "G", [], lambda: g.iota(T.pi[:, 0:1], [[0, 1]], 0, 1))
+    op("ee", "G", [], lambda: g.iota(T.ee[:, :], [[1, 144]], 0, -1, **small))
+    op("uu", "G", [], lambda: g.iota(T.uu[:, :], [[1, 2 * RO]], 1 - RO, 0, **small))
+    op("base", "G", [], lambda: g.iota(T.base[:, :], [[0, NM * S]], int(B), 0, **small))
+    op("one", "V", [], lambda: V.memset(T.one[:, :], 1.0))
+    op("cw0", "V", [], lambda: V.memset(T.cw[0:32, :], (B + 128) / 32))
+    op("cw", "V", [], lambda: V.memset(T.cw[32:64, :], 7.5 / 32))
+    op("ci", "V", [], lambda: V.memset(T.ci[0:32, :], 8.5 / 32))
+    op("pm", "V", ["pi"], lambda: V.tensor_scalar(T.pi[:, 4:5], T.pi[:, 0:1], 15, None, A.bitwise_and))
+    op("pmf", "V", ["pm"], lambda: V.tensor_copy(T.col[:, 0:1], T.pi[:, 4:5]))
+    op("idf", "V", ["ee"], lambda: V.tensor_scalar(T.idf[:, :], T.ee[:, 0:128], 0.0, None, A.is_equal))
+    op("idp", "V", ["ee"], lambda: V.tensor_scalar(T.idp[:, :], T.ee[:, 0:128], 0.0, None, A.is_equal))
+    op("dd", "V", ["pmf", "ee"], lambda: V.tensor_scalar(T.dd[:, :], T.ee[:, :], T.col[:, 0:1], None, A.add))
+    op("cs", "V", ["pmf"], lambda: V.tensor_scalar(T.col[:, 1:2], T.col[:, 0:1], 1.0, 16 * (B + 7.5), A.is_ge, A.mult))
+    op("kc", "V", ["cs", "uu"], lambda: V.tensor_scalar(T.kc[:, :], T.uu[:, :], T.col[:, 1:2], None, A.mult))
+    op("d1", "V", ["dd"], lambda: V.tensor_scalar(T.d1[:, :], T.dd[:, 0:128], 16.0, -128.0, A.is_ge, A.mult))
+    op("d2", "V", ["d1"], lambda: V.tensor_tensor(T.d2[:, :], T.dd[:, 0:128], T.d1[:, :], A.add))
+    op("qw", "V", ["dd"], lambda: V.tensor_scalar(T.qw[:, :], T.dd[:, :], 16.0, -1.0, A.is_equal, A.mult))
+
+    def xsel(s):
+        return lambda: V.tensor_scalar(T.xsel[:, s * 128:(s + 1) * 128], T.d2[:, :], float(s), None,
+                                       A.is_ge if s else A.is_equal)
+    for s in range(S):
+        op(("xsel", s), "V", ["d2"], xsel(s))
+    op("ab", "S", ["ee"], lambda: Sc.activation(T.ab[:, :], T.ee[:, 0:128], F.Abs, bias=48.0))
+    op("ad", "S", ["dd"], lambda: Sc.activation(T.ad[:, :], T.dd[:, 0:128], F.Abs, bias=48.0))
+    op("shp", "V", ["ab"], lambda: V.tensor_scalar(T.shp[:, :], T.ab[:, :], 64.0, None, A.is_equal))
+    op("sh0", "V", ["ad"], lambda: V.tensor_scalar(T.sh0[:, :], T.ad[:, :], 64.0, None, A.is_equal))
+    op("off0", "V", ["place"], lambda: V.tensor_copy(T.off[:, :], T.plc[:, :]))
+    op("plf", "V", ["place", "kc"],
+       lambda: V.tensor_scalar(T.plf[:, :], T.plc[:, :], T.kc[:, 2 * RO - 1:2 * RO], None, A.add))
+
+    def step(c, t):
+        n, a = NS[c], LO[c]
+        b = a + n
+        v = (V0 if t == 0 else VS)[c]
+        last = t == RO - 1
+        m = t * C + c
+        pc_, pin_, acc_ = T["pc%d" % c][:, 0:n], T["pin%d" % (m % 2)][:, 0:n], T["acc%d" % (m % 2)][:, 0:n]
+        back = lambda k, d: [(k, (m - d) % C, (m - d) // C)] if m >= d else []
+        slot = lambda buf, s: buf[:, a * S + s:b * S:S]
+        came = T.land[:, t * J + a:t * J + b]
+        made = T.cb[:, t * J + a:t * J + b]
+        piece = [i for i in range(len(EXT)) if EXT[i][0] <= t <= EXT[i][1]]
+        wide = W + (GROW * EXT[piece[0]][1] if piece else 0)
+        pre = ["ring", "off0"] if t == 0 else [("conv", c, t - 1), ("ext", piece[0])]
+        gathers = []
+        if v < n:
+            op(("gS", c, t), "S", pre,
+               lambda: Sc.activation(T.xb[:, (a + v) * S:b * S], T.win[:, 0:wide].indirect(T.off[:, a + v:b]), F.Copy))
+            gathers.append(("gS", c, t))
+        if v:
+            op(("gV", c, t), "V", pre,
+               lambda: V.tensor_copy(T.xb[:, a * S:(a + v) * S], T.win[:, 0:wide].indirect(T.off[:, a:a + v])))
+            gathers.append(("gV", c, t))
+
+        def p15():
+            P.matmul(pc_, T.cw[0:64, :], T.one[0:64, 0:n], True, False)
+            return P.matmul(pc_, T.idp[:, :], slot(T.xb, S - 1), False, False)
+        op(("p15", c, t), "P", gathers + back("ev", C) + ["cw", "one", "idp"], p15)
+        op(("z", c, t), "G", [("p15", c, t)], lambda: g.iota(slot(T.xb, S - 1), [[0, n]], -int(B) - 128, 0, **small))
+
+        def pin():
+            P.matmul(pin_, T.ci[0:32, :], T.one[0:32, 0:n], True, False)
+            return P.matmul(pin_, (T.shp if t else T.idp)[:, :], came, False, True)
+        op(("pin", c, t), "P", [("arr", c, t - 1) if t else "carry", "ci", "shp", "one", "idp"] + back("ins", 2), pin)
+        op(("ins", c, t), "V", gathers + [("pin", c, t)],
+           lambda: V.tensor_tensor(slot(T.xb, 0), slot(T.xb, 0), pin_, A.add))
+        op(("scan", c, t), "V", [("ins", c, t), ("z", c, t), "base"] + ([("pq", c, t - 1)] if t else []),
+           lambda: V.tensor_tensor_scan(T.qb[:, a * S:b * S], T.base[:, 0:n * S], T.xb[:, a * S:b * S], 0.0, A.max, A.add))
+
+        def px():
+            if last:
+                P.matmul(acc_, T.idf[:, :], T.plf[:, a:b], True, False)
+            r = P.matmul(acc_, T.sh0[:, :] if t else T.xsel[:, 0:128], came, not last, False)
+            for s in range(S - 1, 0, -1):
+                r = P.matmul(acc_, T.xsel[:, s * 128:(s + 1) * 128], slot(T.xb, s - 1), False, False)
+            return r
+        op(("px", c, t), "P", [("ins", c, t), ("xsel", S - 1), "sh0", "idf"]
+           + back("conv" if m - 2 >= (RO - 1) * C else "add", 2), px)
+        op(("pc", c, t), "P", [("scan", c, t)], lambda: P.matmul(pc_, T.idp[:, :], slot(T.qb, S - 1), False, True))
+
+        def pq():
+            for k in range(1, S):
+                r = P.matmul(acc_, T.qw[:, S - k:S - k + 128], slot(T.qb, k - 1), False, k == S - 1)
+            return r
+        op(("pq", c, t), "P", [("scan", c, t), "qw"], pq)
+        op(("q16", c, t), "S", [("pc", c, t)] + ([("ev", c, t - 1)] if t else []),
+           lambda: Sc.activation(T.q16[:, a:b], pc_, F.Identity, bias=-7.5))
+        op(("ev", c, t), "V", [("q16", c, t)], lambda: V.tensor_tensor(made, pc_, T.q16[:, a:b], A.subtract))
+        if not last:
+            op(("add", c, t), "V", [("pq", c, t), "plf"],
+               lambda: V.tensor_tensor(T.plf[:, a:b], T.plf[:, a:b], acc_, A.add))
+            op(("conv", c, t), "V", [("add", c, t), "kc"],
+               lambda: V.tensor_scalar(T.off[:, a:b], T.plf[:, a:b], T.kc[:, t:t + 1], None, A.add))
+            dst = T.cores[(rank + 1 + t % (N - 1)) % N]
+            src = T.cores[(rank - 1 - t % (N - 1)) % N]
+            rid, pid = topo.addr(dst)[0:2]
+            name = "arr%d_%d" % (c, t)
+            op(("rem", c, t), "G", [("ev", c, t)],
+               lambda: g.remote_dma(T.land[:, (t + 1) * J + a:(t + 1) * J + b], made,
+                                    T.sem[name], T.sem.sent, pid, rid, topo.mask(core, dst)),
+               "sent", len(topo.engines(core, dst)))
+            op(("arr", c, t), None, [], None, name, len(topo.engines(src, core)))
+        else:
+            op(("add", c, t), "V", [("pq", c, t)],
+               lambda: V.tensor_scalar(T.msk[:, a:b], acc_, float(W), -float(W), A.is_ge, A.mult))
+            op(("conv", c, t), "V", [("add", c, t)],
+               lambda: V.tensor_tensor(T.ypo[:, a:b], acc_, T.msk[:, a:b], A.add))
+            if c >= C - 2:
+                lo = a if c == C - 1 else 0
+                op(("yp", c), "Y", [("conv", c, t)], lambda: Y.dma_start(T.yp[:, lo:b], T.ypo[:, lo:b]), "out", 16)
+                op(("ycl", c), "Y", [("ev", c, t)],
+                   lambda: Y.dma_start(T.yc[:, t * J + lo:t * J + b], T.cb[:, t * J + lo:t * J + b]), "out", 16)
+    for t in range(RO):
+        for c in range(C):
+            step(c, t)
+
+    def store(i):
+        a, b = YB[i][0] * J, (YB[i][1] + 1) * J
+        return lambda: Y.dma_start(T.yc[:, a:b], T.cb[:, a:b])
+    for i in range(len(YB)):
+        op(("yc", i), "Y", [("ev", c, YB[i][1]) for c in range(C)], store(i), "out", 16)
+
+    late = [(("ext", i), EXT[i][0] - 3) for i in range(1, len(EXT))] + [(("yc", i), YB[i][1]) for i in range(len(YB))]
+    late.sort(key=lambda e: e[1])
+    order = {
+        "G": ["pi", "ee", "uu", "base"] + periodic(PAT_G, ops),
+        "V": ["one", "cw0", "cw", "ci", "pm", "idf", "pmf", "idp", "dd", "cs", "d1", "kc", "d2", "qw", "shp", "sh0"]
+             + [("xsel", s) for s in range(S // 2)] + ["off0", "plf"] + [("xsel", s) for s in range(S // 2, S)]
+             + periodic(PAT_V, ops),
+        "S": ["place", "ab", "ad"] + periodic(PAT_S, ops),
+        "P": periodic(PAT_P, ops),
+        "Y": ["ring", "carry", ("ext", 0)] + [e[0] for e in late]
+             + [x for c in (C - 2, C - 1) for x in (("ycl", c), ("yp", c))],
+    }
+
+    total, at = {}, {}
+    for q in order:
+        for name in order[q]:
+            sem, inc = ops[name][3], ops[name][4]
+            total[sem] = total.get(sem, 0) + inc
+            at[name] = total[sem]
+    known = {q: {} for q in order}
+    clock = {}
+    for name in ops:
+        if ops[name][0] is None:
+            at[name] = total[ops[name][3]] = ops[name][4]
+            clock[name] = {ops[name][3]: at[name]}
+    waited = {}
+    calls = {q: [] for q in order}
+    pos = {q: 0 for q in order}
+    left = sum(len(x) for x in order.values())
+    while left:
+        before = left
+        for q in order:
+            while pos[q] < len(order[q]) and all(d in clock for d in ops[order[q][pos[q]]][1]):
+                name = order[q][pos[q]]
+                deps = ops[name][1]
+                deps = [d for d in deps if not any(e != d and clock[e].get(ops[d][3], 0) >= at[d] for e in deps)]
+                waits = []
+                for d in deps:
+                    sem = ops[d][3]
+                    if known[q].get(sem, 0) < at[d]:
+                        waits.append((sem, at[d]))
+                        waited[sem] = max(waited.get(sem, 0), at[d])
+                        for k, val in clock[d].items():
+                            known[q][k] = max(known[q].get(k, 0), val)
+                clock[name] = dict(known[q])
+                clock[name][ops[name][3]] = at[name]
+                calls[q].append((waits, name))
+                pos[q] += 1
+                left -= 1
+        assert left < before, "the queues' orders wait for one another"
+    for q in order:
+        for waits, name in calls[q]:
+            for sem, val in waits:
+                queue[q].wait_ge(T.sem[sem], val)
+            r = ops[name][2]()
+            if ops[name][3] != "sent":
+                r.then_inc(T.sem[ops[name][3]], ops[name][4])
+    for sem in total:
+        if waited.get(sem, 0) < total[sem]:
+            (Y if sem == "out" else g).wait_ge(T.sem[sem], total[sem])

@@ -4,16 +4,15 @@ W, S, J, RO = 4096, 16, 256, 12
 GROW = 15 * 16
 B = 3072.0
 NS = [64, 64, 64, 64]
-VS = [18, 18, 18, 18]
-V0 = [32, 18, 18, 18]
+VS = [16, 16, 16, 16]
+V0 = [32, 16, 16, 16]
 C = len(NS)
 NM = max(NS)
 LO = [sum(NS[:c]) for c in range(C)]
-EXT = [(1, 3), (4, 7), (8, 11)]
-YB = [(0, 3), (4, 7), (8, 10)]
-PAT_V = [("scan", 0), ("add", -1), ("gV", 2), ("conv", -1), ("ins", 1), ("ev", 0)]
-PAT_S = [("q16", 0), ("gS", 2)]
-PAT_P = [("pc", 0), ("p15", 1), ("pin", 1), ("pq", 0), ("px", 1)]
+EXT = [(1, 2), (3, 11)]
+PAT_V = [("conv", -2), ("scan", 0), ("gV", 2), ("q16", 0), ("add", -1), ("ins", 1), ("ev", 0)]
+PAT_S = [("gS", 2), ("fix", -1)]
+PAT_P = [("px", 0), ("p15", 1), ("pc", 0), ("pa", 1), ("pq", 0)]
 PAT_G = [("rem", 0), ("z", 2)]
 
 SCRATCH = {
@@ -38,22 +37,19 @@ SCRATCH = {
     "d1": ("sbuf", [128, 128], "bfloat16"),
     "d2": ("sbuf", [128, 128], "bfloat16"),
     "ab": ("sbuf", [128, 128], "bfloat16"),
-    "ad": ("sbuf", [128, 128], "bfloat16"),
+    "ycb": ("sbuf", [128, (RO - 1) * J], "bfloat16"),
     "qw": ("sbuf", [128, 144], "bfloat16"),
     "xsel": ("sbuf", [128, S * 128], "bfloat16"),
     "shp": ("sbuf", [128, 128], "bfloat16"),
-    "sh0": ("sbuf", [128, 128], "bfloat16"),
     "idp": ("sbuf", [128, 128], "bfloat16"),
     "idf": ("sbuf", [128, 128], "float32"),
     "one": ("sbuf", [128, NM], "bfloat16"),
     "cw": ("sbuf", [128, 128], "bfloat16"),
     "ci": ("sbuf", [128, 128], "bfloat16"),
 }
-for _c in range(C):
+for _c in range(3):
     SCRATCH["pc%d" % _c] = ("psum", [128, 512], "float32")
-for _c in range(2):
     SCRATCH["acc%d" % _c] = ("psum", [128, 512], "float32")
-    SCRATCH["pin%d" % _c] = ("psum", [128, 512], "float32")
 
 SEMAPHORES = (["cV", "cS", "cP", "cG", "ring", "place", "carry", "sent", "out"]
               + ["ext%d" % i for i in range(len(EXT))]
@@ -92,7 +88,7 @@ def rank_program(g, core, T, topo):
         a, b = GROW * (EXT[i][0] - 1), GROW * EXT[i][1]
         return lambda: Y.dma_start(T.win[:, W + a:W + b], T.ring[:, a:b])
     for i in range(len(EXT)):
-        op(("ext", i), "Y", ["ring"] if i == 0 else [("ev", C - 1, EXT[i][0] - 3)], ext(i), "ext%d" % i, 16)
+        op(("ext", i), "Y", ["ring"], ext(i), "ext%d" % i, 16)
 
     op("pi", "G", [], lambda: g.iota(T.pi[:, 0:1], [[0, 1]], 0, 1))
     op("ee", "G", [], lambda: g.iota(T.ee[:, :], [[1, 144]], 0, -1, **small))
@@ -101,13 +97,15 @@ def rank_program(g, core, T, topo):
     op("one", "V", [], lambda: V.memset(T.one[:, :], 1.0))
     op("cw0", "V", [], lambda: V.memset(T.cw[0:32, :], (B + 128) / 32))
     op("cw", "V", [], lambda: V.memset(T.cw[32:64, :], 7.5 / 32))
-    op("ci", "V", [], lambda: V.memset(T.ci[0:32, :], 8.5 / 32))
+    op("ci", "V", [], lambda: V.memset(T.ci[0:32, :], (B + 144) / 32))
+    op("c85", "V", ["carry"], lambda: V.tensor_scalar(T.land[:, 0:J], T.land[:, 0:J], 8.5, None, A.add))
     op("pm", "V", ["pi"], lambda: V.tensor_scalar(T.pi[:, 4:5], T.pi[:, 0:1], 15, None, A.bitwise_and))
     op("pmf", "V", ["pm"], lambda: V.tensor_copy(T.col[:, 0:1], T.pi[:, 4:5]))
     op("idf", "V", ["ee"], lambda: V.tensor_scalar(T.idf[:, :], T.ee[:, 0:128], 0.0, None, A.is_equal))
     op("idp", "V", ["ee"], lambda: V.tensor_scalar(T.idp[:, :], T.ee[:, 0:128], 0.0, None, A.is_equal))
     op("dd", "V", ["pmf", "ee"], lambda: V.tensor_scalar(T.dd[:, :], T.ee[:, :], T.col[:, 0:1], None, A.add))
-    op("cs", "V", ["pmf"], lambda: V.tensor_scalar(T.col[:, 1:2], T.col[:, 0:1], 1.0, 16 * (B + 7.5), A.is_ge, A.mult))
+    op("cs1", "V", ["pmf"], lambda: V.tensor_scalar(T.col[:, 2:3], T.col[:, 0:1], 1.0, 16 * (B + 16), A.is_ge, A.mult))
+    op("cs", "V", ["cs1"], lambda: V.tensor_scalar(T.col[:, 1:2], T.col[:, 2:3], -16 * 8.5, None, A.add))
     op("kc", "V", ["cs", "uu"], lambda: V.tensor_scalar(T.kc[:, :], T.uu[:, :], T.col[:, 1:2], None, A.mult))
     op("d1", "V", ["dd"], lambda: V.tensor_scalar(T.d1[:, :], T.dd[:, 0:128], 16.0, -128.0, A.is_ge, A.mult))
     op("d2", "V", ["d1"], lambda: V.tensor_tensor(T.d2[:, :], T.dd[:, 0:128], T.d1[:, :], A.add))
@@ -119,9 +117,7 @@ def rank_program(g, core, T, topo):
     for s in range(S):
         op(("xsel", s), "V", ["d2"], xsel(s))
     op("ab", "S", ["ee"], lambda: Sc.activation(T.ab[:, :], T.ee[:, 0:128], F.Abs, bias=48.0))
-    op("ad", "S", ["dd"], lambda: Sc.activation(T.ad[:, :], T.dd[:, 0:128], F.Abs, bias=48.0))
     op("shp", "V", ["ab"], lambda: V.tensor_scalar(T.shp[:, :], T.ab[:, :], 64.0, None, A.is_equal))
-    op("sh0", "V", ["ad"], lambda: V.tensor_scalar(T.sh0[:, :], T.ad[:, :], 64.0, None, A.is_equal))
     op("off0", "V", ["place"], lambda: V.tensor_copy(T.off[:, :], T.plc[:, :]))
     op("plf", "V", ["place", "kc"],
        lambda: V.tensor_scalar(T.plf[:, :], T.plc[:, :], T.kc[:, 2 * RO - 1:2 * RO], None, A.add))
@@ -132,7 +128,8 @@ def rank_program(g, core, T, topo):
         v = (V0 if t == 0 else VS)[c]
         last = t == RO - 1
         m = t * C + c
-        pc_, pin_, acc_ = T["pc%d" % c][:, 0:n], T["pin%d" % (m % 2)][:, 0:n], T["acc%d" % (m % 2)][:, 0:n]
+        pc_, acc_ = T["pc%d" % (m % 3)][:, 0:n], T["acc%d" % (m % 3)][:, 0:n]
+        move = (T.idp if last else T.shp)[:, :]
         back = lambda k, d: [(k, (m - d) % C, (m - d) // C)] if m >= d else []
         slot = lambda buf, s: buf[:, a * S + s:b * S:S]
         came = T.land[:, t * J + a:t * J + b]
@@ -151,44 +148,50 @@ def rank_program(g, core, T, topo):
             gathers.append(("gV", c, t))
 
         def p15():
-            P.matmul(pc_, T.cw[0:64, :], T.one[0:64, 0:n], True, False)
-            return P.matmul(pc_, T.idp[:, :], slot(T.xb, S - 1), False, False)
-        op(("p15", c, t), "P", gathers + back("ev", C) + ["cw", "one", "idp"], p15)
+            if last:
+                P.matmul(pc_, T.cw[0:64, :], T.one[0:64, 0:n], True, False)
+            else:
+                P.matmul(pc_, T.ci[0:32, :], T.one[0:32, 0:n], True, False)
+            return P.matmul(pc_, move, slot(T.xb, S - 1), False, False)
+        op(("p15", c, t), "P", gathers + back("ev", 3) + ["cw", "ci", "one", "idp", "shp"], p15)
         op(("z", c, t), "G", [("p15", c, t)], lambda: g.iota(slot(T.xb, S - 1), [[0, n]], -int(B) - 128, 0, **small))
 
-        def pin():
-            P.matmul(pin_, T.ci[0:32, :], T.one[0:32, 0:n], True, False)
-            return P.matmul(pin_, (T.shp if t else T.idp)[:, :], came, False, True)
-        op(("pin", c, t), "P", [("arr", c, t - 1) if t else "carry", "ci", "shp", "one", "idp"] + back("ins", 2), pin)
-        op(("ins", c, t), "V", gathers + [("pin", c, t)],
-           lambda: V.tensor_tensor(slot(T.xb, 0), slot(T.xb, 0), pin_, A.add))
+        op(("ins", c, t), "V", gathers + [("arr", c, t - 1) if t else "c85"],
+           lambda: V.tensor_tensor(slot(T.xb, 0), slot(T.xb, 0), came, A.add))
         op(("scan", c, t), "V", [("ins", c, t), ("z", c, t), "base"] + ([("pq", c, t - 1)] if t else []),
            lambda: V.tensor_tensor_scan(T.qb[:, a * S:b * S], T.base[:, 0:n * S], T.xb[:, a * S:b * S], 0.0, A.max, A.add))
 
-        def px():
+        def pa():
             if last:
                 P.matmul(acc_, T.idf[:, :], T.plf[:, a:b], True, False)
-            r = P.matmul(acc_, T.sh0[:, :] if t else T.xsel[:, 0:128], came, not last, False)
-            for s in range(S - 1, 0, -1):
-                r = P.matmul(acc_, T.xsel[:, s * 128:(s + 1) * 128], slot(T.xb, s - 1), False, False)
+            for s in range(S - 1, 1, -1):
+                r = P.matmul(acc_, T.xsel[:, s * 128:(s + 1) * 128], slot(T.xb, s - 1), s == S - 1 and not last, False)
             return r
-        op(("px", c, t), "P", [("ins", c, t), ("xsel", S - 1), "sh0", "idf"]
-           + back("conv" if m - 2 >= (RO - 1) * C else "add", 2), px)
-        op(("pc", c, t), "P", [("scan", c, t)], lambda: P.matmul(pc_, T.idp[:, :], slot(T.qb, S - 1), False, True))
+        op(("pa", c, t), "P", gathers + [("xsel", S - 1), "idf"]
+           + back("conv" if m - 3 >= (RO - 1) * C else "add", 3), pa)
+
+        def px():
+            P.matmul(acc_, T.xsel[:, 0:128], came, False, False)
+            return P.matmul(acc_, T.xsel[:, 128:256], slot(T.xb, 0), False, False)
+        op(("px", c, t), "P", [("ins", c, t)], px)
+        op(("pc", c, t), "P", [("scan", c, t)], lambda: P.matmul(pc_, move, slot(T.qb, S - 1), False, True))
 
         def pq():
             for k in range(1, S):
                 r = P.matmul(acc_, T.qw[:, S - k:S - k + 128], slot(T.qb, k - 1), False, k == S - 1)
             return r
         op(("pq", c, t), "P", [("scan", c, t), "qw"], pq)
-        op(("q16", c, t), "S", [("pc", c, t)] + ([("ev", c, t - 1)] if t else []),
-           lambda: Sc.activation(T.q16[:, a:b], pc_, F.Identity, bias=-7.5))
+        op(("q16", c, t), "V", [("pc", c, t)] + ([("ev", c, t - 1)] if t else []),
+           lambda: V.tensor_scalar(T.q16[:, a:b], pc_, -7.5 if last else -16.0, None, A.add))
         op(("ev", c, t), "V", [("q16", c, t)], lambda: V.tensor_tensor(made, pc_, T.q16[:, a:b], A.subtract))
         if not last:
             op(("add", c, t), "V", [("pq", c, t), "plf"],
                lambda: V.tensor_tensor(T.plf[:, a:b], T.plf[:, a:b], acc_, A.add))
             op(("conv", c, t), "V", [("add", c, t), "kc"],
                lambda: V.tensor_scalar(T.off[:, a:b], T.plf[:, a:b], T.kc[:, t:t + 1], None, A.add))
+            if c == C - 1:
+                op(("fix", c, t), "S", [("ev", c, t)],
+                   lambda: Sc.activation(T.ycb[:, t * J:(t + 1) * J], T.cb[:, t * J:(t + 1) * J], F.Identity, bias=-8.5))
             dst = T.cores[(rank + 1 + t % (N - 1)) % N]
             src = T.cores[(rank - 1 - t % (N - 1)) % N]
             rid, pid = topo.addr(dst)[0:2]
@@ -212,22 +215,17 @@ def rank_program(g, core, T, topo):
         for c in range(C):
             step(c, t)
 
-    def store(i):
-        a, b = YB[i][0] * J, (YB[i][1] + 1) * J
-        return lambda: Y.dma_start(T.yc[:, a:b], T.cb[:, a:b])
-    for i in range(len(YB)):
-        op(("yc", i), "Y", [("ev", c, YB[i][1]) for c in range(C)], store(i), "out", 16)
-
-    late = [(("ext", i), EXT[i][0] - 3) for i in range(1, len(EXT))] + [(("yc", i), YB[i][1]) for i in range(len(YB))]
-    late.sort(key=lambda e: e[1])
+    done = [("fix", C - 1, RO - 2), ("rem", C - 1, RO - 2)]
+    op(("yc", 0), "Y", done, lambda: Y.dma_start(T.yc[0:112, 0:(RO - 1) * J], T.ycb[16:128, :]), "out", 16)
+    op(("yc", 1), "Y", done, lambda: Y.dma_start(T.yc[112:128, 0:(RO - 1) * J], T.ycb[0:16, :]), "out", 16)
     order = {
         "G": ["pi", "ee", "uu", "base"] + periodic(PAT_G, ops),
-        "V": ["one", "cw0", "cw", "ci", "pm", "idf", "pmf", "idp", "dd", "cs", "d1", "kc", "d2", "qw", "shp", "sh0"]
+        "V": ["one", "cw0", "cw", "ci", "pm", "idf", "pmf", "idp", "dd", "cs1", "d1", "cs", "d2", "kc", "qw", "shp"]
              + [("xsel", s) for s in range(S // 2)] + ["off0", "plf"] + [("xsel", s) for s in range(S // 2, S)]
-             + periodic(PAT_V, ops),
-        "S": ["place", "ab", "ad"] + periodic(PAT_S, ops),
+             + periodic(PAT_V, ops)[:1] + ["c85"] + periodic(PAT_V, ops)[1:],
+        "S": ["place", "ab"] + periodic(PAT_S, ops),
         "P": periodic(PAT_P, ops),
-        "Y": ["ring", "carry", ("ext", 0)] + [e[0] for e in late]
+        "Y": ["ring", "carry"] + [("ext", i) for i in range(len(EXT))] + [("yc", 0), ("yc", 1)]
              + [x for c in (C - 2, C - 1) for x in (("ycl", c), ("yp", c))],
     }
 

@@ -1,76 +1,112 @@
+from concourse.bass import DstId, RemoteDMATransfer
 from concourse.mybir import AluOpType as A, ActivationFunctionType as F
 
 W, S, J, RO = 4096, 16, 256, 12
 GROW = 15 * 16
 B = 3072.0
+BW = 1.5 * 128 * W
+BF = 1.5 * 2 ** 27
+PAD = 16
+VIA = [(t, min(t + 2, RO - 1)) for t in range(0, RO - 1, 2)]
 NS = [64, 64, 64, 64]
-VS = [16, 16, 16, 16]
-V0 = [32, 16, 16, 16]
+VS = [16, 16, 14, 16]
+V0 = [32, 30, 16, 16]
+VL = [14, 16, 14, 14]
 C = len(NS)
 NM = max(NS)
 LO = [sum(NS[:c]) for c in range(C)]
 EXT = [(1, 2), (3, 11)]
-PAT_V = [("conv", -2), ("scan", 0), ("gV", 2), ("q16", 0), ("add", -1), ("ins", 1), ("ev", 0)]
-PAT_S = [("gS", 2), ("fix", -1)]
-PAT_P = [("px", 0), ("p15", 1), ("pc", 0), ("pa", 1), ("pq", 0)]
-PAT_G = [("rem", 0), ("z", 2)]
+PAT_V = [("scan", 0), ("add", -1), ("fin", -2), ("gV", 2), ("z", 1), ("lack", -1), ("rnd", -1), ("ins", 1), ("q16", 0), ("ev", 0)]
+HEAD_P = [("p15", 0, 0), ("pa", 0, 0), ("p15", 1, 0), ("pa", 1, 0)]
+TAIL_V = [("scan", 3, 11), ("add", 2, 11), ("fin", 1, 11), ("q16", 3, 11), ("fin", 2, 11), ("ev", 3, 11), ("rnd", 3, 11), ("fin", 3, 11)]
+PAT_S = [("gS", 3), ("rnd", -1)]
+PAT_P = [("p15", 1), ("pc", 0), ("px", 0), ("pq", 0), ("pa", 1)]
+PAT_G = [("rem", -1), ("z", 1), ("sum", -1)]
 
 SCRATCH = {
-    "win": ("sbuf", [128, W + GROW * (RO - 1)], "bfloat16"),
+    "win": ("sbuf", [128, PAD + W + GROW * (RO - 1)], "bfloat16"),
     "xb": ("sbuf", [128, J * S], "bfloat16"),
     "qb": ("sbuf", [128, J * S], "bfloat16"),
-    "base": ("sbuf", [128, NM * S], "bfloat16"),
+    "nil": ("sbuf", [128, NM * S], "bfloat16"),
+    "base": ("sbuf", [128, NM * S], "float16"),
     "land": ("sbuf", [128, RO * J], "bfloat16"),
     "cb": ("sbuf", [128, RO * J], "bfloat16"),
-    "q16": ("sbuf", [128, J], "bfloat16"),
+    "pb": ("sbuf", [128, RO * J], "bfloat16"),
+    "nq": ("sbuf", [128, RO * J], "bfloat16"),
     "off": ("sbuf", [128, J], "uint16"),
     "plc": ("sbuf", [128, J], "int32"),
     "plf": ("sbuf", [128, J], "float32"),
-    "msk": ("sbuf", [128, J], "float32"),
+    "msk": ("sbuf", [128, J], "bfloat16"),
     "ypo": ("sbuf", [128, J], "float32"),
     "pi": ("sbuf", [128, 8], "int32"),
     "col": ("sbuf", [128, 8], "float32"),
-    "uu": ("sbuf", [128, 2 * RO], "float32"),
-    "kc": ("sbuf", [128, 2 * RO], "float32"),
+    "raw": ("sbuf", [128, J], "bfloat16"),
+    "ofk": ("sbuf", [128, J], "uint16"),
+    "plk": ("sbuf", [128, J], "float32"),
     "ee": ("sbuf", [128, 144], "bfloat16"),
     "dd": ("sbuf", [128, 144], "bfloat16"),
     "d1": ("sbuf", [128, 128], "bfloat16"),
     "d2": ("sbuf", [128, 128], "bfloat16"),
     "ab": ("sbuf", [128, 128], "bfloat16"),
-    "ycb": ("sbuf", [128, (RO - 1) * J], "bfloat16"),
+    "half": ("sbuf", [128, 2 * J], "bfloat16"),
     "qw": ("sbuf", [128, 144], "bfloat16"),
     "xsel": ("sbuf", [128, S * 128], "bfloat16"),
-    "shp": ("sbuf", [128, 128], "bfloat16"),
+    "shn": ("sbuf", [128, 128], "bfloat16"),
     "idp": ("sbuf", [128, 128], "bfloat16"),
     "idf": ("sbuf", [128, 128], "float32"),
     "one": ("sbuf", [128, NM], "bfloat16"),
     "cw": ("sbuf", [128, 128], "bfloat16"),
-    "ci": ("sbuf", [128, 128], "bfloat16"),
 }
-for _c in range(3):
+for _c in range(C):
     SCRATCH["pc%d" % _c] = ("psum", [128, 512], "float32")
     SCRATCH["acc%d" % _c] = ("psum", [128, 512], "float32")
 
-SEMAPHORES = (["cV", "cS", "cP", "cG", "ring", "place", "carry", "sent", "out"]
+SEMAPHORES = (["cV", "cS", "cP", "cG", "ring", "place", "carry", "sent", "out", "lent", "back", "late"]
+              + ["got%d" % i for i in range(len(VIA))]
               + ["ext%d" % i for i in range(len(EXT))]
               + ["arr%d_%d" % (c, t) for c in range(C) for t in range(RO - 1)])
 
 
-def periodic(pat, ops):
+def periodic(pat, ops, q):
     seq = []
-    for m in range(-C, (RO + 1) * C):
+    for m in range(-2 * C, (RO + 2) * C):
         for k, d in pat:
-            x = m + d
-            if 0 <= x < RO * C and (k, x % C, x // C) in ops:
-                seq.append((k, x % C, x // C))
+            name = (k, (m + d) % C, (m + d) // C)
+            if name in ops and ops[name][0] == q:
+                seq.append(name)
     return seq
+
+
+def helper_of(core, cores, topo):
+    return [c for c in topo.cores_of(core) if c not in cores and topo.die(c) == topo.die(core)][0]
+
+
+def hand_back(g, core, owner, T, topo):
+    rid, pid = topo.addr(owner)[0:2]
+    off_chip = topo.mask(owner, [c for c in T.cores if c != owner][0])
+    for i, (u, w) in enumerate(VIA):
+        g.wait_ge(T.sem["got%d" % i], bin(topo.mask(owner, core) & ~off_chip).count("1"))
+        piece = T.cb[:, u * J:w * J]
+        g.remote_dma(piece, piece, T.sem["late" if w == RO - 1 else "back"], T.sem.lent, pid, rid, topo.mask(core, owner))
+    g.wait_ge(T.sem.lent, len(VIA) * len(topo.engines(core, owner)))
 
 
 def rank_program(g, core, T, topo):
     rank = T.rank_of(core)
     if rank is None:
+        for owner in T.cores:
+            if helper_of(owner, T.cores, topo) == core:
+                hand_back(g, core, owner, T, topo)
         return
     N = len(T.cores)
+    aid = helper_of(core, T.cores, topo)
+    spare = topo.mask(core, aid) & ~topo.mask(core, T.cores[(rank + 1) % N])
+
+    def fold(dst, mask, there, here, srcs, out):
+        rid, pid = topo.addr(dst)[0:2]
+        return g.remote_dma_fused([RemoteDMATransfer(
+            dst_ids=[DstId(rid=rid, pnc=pid)], dma_engine_mask=mask, remote_sem=T.sem[there],
+            srcs=srcs, dsts=[out], alu_op=1)], local_sem=T.sem[here])
     V, Sc, P, Y = g.vector, g.scalar, g.tensor, g.sync
     queue = {"V": V, "S": Sc, "P": P, "G": g, "Y": Y}
     ops = {}
@@ -80,33 +116,31 @@ def rank_program(g, core, T, topo):
 
     small = dict(allow_small_or_imprecise_dtypes=True)
 
-    op("ring", "Y", [], lambda: Y.dma_start(T.win[:, 0:W], T.ring[:, :]), "ring", 16)
+    op("ring", "Y", [], lambda: Y.dma_start(T.win[:, PAD:PAD + W], T.ring[:, :]), "ring", 16)
     op("place", "S", [], lambda: Sc.dma_start(T.plc[:, :], T.place[:, :]), "place", 16)
-    op("carry", "Y", [], lambda: Y.dma_start(T.land[:, 0:J], T.carry[:, :]), "carry", 16)
+    op("carry", "S", [], lambda: Sc.dma_start(T.raw[:, :], T.carry[:, :]), "carry", 16)
 
     def ext(i):
         a, b = GROW * (EXT[i][0] - 1), GROW * EXT[i][1]
-        return lambda: Y.dma_start(T.win[:, W + a:W + b], T.ring[:, a:b])
+        return lambda: Y.dma_start(T.win[:, PAD + W + a:PAD + W + b], T.ring[:, a:b])
     for i in range(len(EXT)):
         op(("ext", i), "Y", ["ring"], ext(i), "ext%d" % i, 16)
 
     op("pi", "G", [], lambda: g.iota(T.pi[:, 0:1], [[0, 1]], 0, 1))
     op("ee", "G", [], lambda: g.iota(T.ee[:, :], [[1, 144]], 0, -1, **small))
-    op("uu", "G", [], lambda: g.iota(T.uu[:, :], [[1, 2 * RO]], 1 - RO, 0, **small))
-    op("base", "G", [], lambda: g.iota(T.base[:, :], [[0, NM * S]], int(B), 0, **small))
+    op("nil", "G", [], lambda: g.iota(T.nil[:, :], [[0, NM * S]], 0, 0, **small))
+    op("base", "G", ["nil"], lambda: g.affine_select(T.base[:, :], T.nil[:, :], [[0, NM * S]], A.is_gt, B + 8, 0, 0))
     op("one", "V", [], lambda: V.memset(T.one[:, :], 1.0))
+    op("half", "V", [], lambda: V.memset(T.half[:, :], -0.5))
     op("cw0", "V", [], lambda: V.memset(T.cw[0:32, :], (B + 128) / 32))
     op("cw", "V", [], lambda: V.memset(T.cw[32:64, :], 7.5 / 32))
-    op("ci", "V", [], lambda: V.memset(T.ci[0:32, :], (B + 144) / 32))
-    op("c85", "V", ["carry"], lambda: V.tensor_scalar(T.land[:, 0:J], T.land[:, 0:J], 8.5, None, A.add))
+    op("c85", "V", ["carry"], lambda: V.tensor_scalar(T.land[:, 0:J], T.raw[:, :], 0.5, None, A.add))
     op("pm", "V", ["pi"], lambda: V.tensor_scalar(T.pi[:, 4:5], T.pi[:, 0:1], 15, None, A.bitwise_and))
     op("pmf", "V", ["pm"], lambda: V.tensor_copy(T.col[:, 0:1], T.pi[:, 4:5]))
     op("idf", "V", ["ee"], lambda: V.tensor_scalar(T.idf[:, :], T.ee[:, 0:128], 0.0, None, A.is_equal))
     op("idp", "V", ["ee"], lambda: V.tensor_scalar(T.idp[:, :], T.ee[:, 0:128], 0.0, None, A.is_equal))
     op("dd", "V", ["pmf", "ee"], lambda: V.tensor_scalar(T.dd[:, :], T.ee[:, :], T.col[:, 0:1], None, A.add))
-    op("cs1", "V", ["pmf"], lambda: V.tensor_scalar(T.col[:, 2:3], T.col[:, 0:1], 1.0, 16 * (B + 16), A.is_ge, A.mult))
-    op("cs", "V", ["cs1"], lambda: V.tensor_scalar(T.col[:, 1:2], T.col[:, 2:3], -16 * 8.5, None, A.add))
-    op("kc", "V", ["cs", "uu"], lambda: V.tensor_scalar(T.kc[:, :], T.uu[:, :], T.col[:, 1:2], None, A.mult))
+    op("cs", "V", ["pmf"], lambda: V.tensor_scalar(T.col[:, 1:2], T.col[:, 0:1], 1.0, 16 * (B + 16), A.is_ge, A.mult))
     op("d1", "V", ["dd"], lambda: V.tensor_scalar(T.d1[:, :], T.dd[:, 0:128], 16.0, -128.0, A.is_ge, A.mult))
     op("d2", "V", ["d1"], lambda: V.tensor_tensor(T.d2[:, :], T.dd[:, 0:128], T.d1[:, :], A.add))
     op("qw", "V", ["dd"], lambda: V.tensor_scalar(T.qw[:, :], T.dd[:, :], 16.0, -1.0, A.is_equal, A.mult))
@@ -117,26 +151,26 @@ def rank_program(g, core, T, topo):
     for s in range(S):
         op(("xsel", s), "V", ["d2"], xsel(s))
     op("ab", "S", ["ee"], lambda: Sc.activation(T.ab[:, :], T.ee[:, 0:128], F.Abs, bias=48.0))
-    op("shp", "V", ["ab"], lambda: V.tensor_scalar(T.shp[:, :], T.ab[:, :], 64.0, None, A.is_equal))
-    op("off0", "V", ["place"], lambda: V.tensor_copy(T.off[:, :], T.plc[:, :]))
-    op("plf", "V", ["place", "kc"],
-       lambda: V.tensor_scalar(T.plf[:, :], T.plc[:, :], T.kc[:, 2 * RO - 1:2 * RO], None, A.add))
+    op("shn", "V", ["ab"], lambda: V.tensor_scalar(T.shn[:, :], T.ab[:, :], 64.0, -1.0, A.is_equal, A.mult))
+    op("pad", "V", [], lambda: V.memset(T.win[:, 0:PAD], 0.0))
+    op("off0", "V", ["place", "pad"], lambda: V.tensor_scalar(T.off[:, :], T.plc[:, :], float(PAD), None, A.add))
+    op("c0", "V", ["pmf"], lambda: V.tensor_scalar(T.col[:, 2:3], T.col[:, 0:1], 1.0, 16 * (B + 16) - 8, A.is_ge, A.mult))
+    op("plk", "V", ["place", "c0"], lambda: V.tensor_scalar(T.ofk[:, :], T.plc[:, :], T.col[:, 2:3], float(PAD), A.add, A.add))
 
     def step(c, t):
         n, a = NS[c], LO[c]
         b = a + n
-        v = (V0 if t == 0 else VS)[c]
         last = t == RO - 1
-        m = t * C + c
-        pc_, acc_ = T["pc%d" % (m % 3)][:, 0:n], T["acc%d" % (m % 3)][:, 0:n]
-        move = (T.idp if last else T.shp)[:, :]
-        back = lambda k, d: [(k, (m - d) % C, (m - d) // C)] if m >= d else []
+        v = (V0 if t == 0 else VL if last else VS)[c]
+        pc_, acc_ = T["pc%d" % c][:, 0:n], T["acc%d" % c][:, 0:n]
+        move = (T.idp if last else T.shn)[:, :]
+        before = lambda k: [(k, c, t - 1)] if t else []
         slot = lambda buf, s: buf[:, a * S + s:b * S:S]
         came = T.land[:, t * J + a:t * J + b]
         made = T.cb[:, t * J + a:t * J + b]
         piece = [i for i in range(len(EXT)) if EXT[i][0] <= t <= EXT[i][1]]
-        wide = W + (GROW * EXT[piece[0]][1] if piece else 0)
-        pre = ["ring", "off0"] if t == 0 else [("conv", c, t - 1), ("ext", piece[0])]
+        wide = PAD + W + (GROW * EXT[piece[0]][1] if piece else 0)
+        pre = ["ring", "off0"] if t == 0 else [("add", c, t - 1), ("ext", piece[0])]
         gathers = []
         if v < n:
             op(("gS", c, t), "S", pre,
@@ -150,28 +184,34 @@ def rank_program(g, core, T, topo):
         def p15():
             if last:
                 P.matmul(pc_, T.cw[0:64, :], T.one[0:64, 0:n], True, False)
-            else:
-                P.matmul(pc_, T.ci[0:32, :], T.one[0:32, 0:n], True, False)
-            return P.matmul(pc_, move, slot(T.xb, S - 1), False, False)
-        op(("p15", c, t), "P", gathers + back("ev", 3) + ["cw", "ci", "one", "idp", "shp"], p15)
-        op(("z", c, t), "G", [("p15", c, t)], lambda: g.iota(slot(T.xb, S - 1), [[0, n]], -int(B) - 128, 0, **small))
+            return P.matmul(pc_, move, slot(T.xb, S - 1), not last, False)
+        op(("p15", c, t), "P", gathers + before("ev") + before("q16") + ["cw", "one", "idp", "shn"], p15)
+        if (c, t) == (2, 0):
+            op(("z", c, t), "V", [("p15", c, t)], lambda: V.memset(slot(T.xb, S - 1), -B - 128))
+        else:
+            op(("z", c, t), "G", [("p15", c, t)], lambda: g.iota(slot(T.xb, S - 1), [[0, n]], -int(B) - 128, 0, **small))
 
         op(("ins", c, t), "V", gathers + [("arr", c, t - 1) if t else "c85"],
            lambda: V.tensor_tensor(slot(T.xb, 0), slot(T.xb, 0), came, A.add))
-        op(("scan", c, t), "V", [("ins", c, t), ("z", c, t), "base"] + ([("pq", c, t - 1)] if t else []),
+        op(("scan", c, t), "V", [("ins", c, t), ("z", c, t), "base"] + before("pq"),
            lambda: V.tensor_tensor_scan(T.qb[:, a * S:b * S], T.base[:, 0:n * S], T.xb[:, a * S:b * S], 0.0, A.max, A.add))
 
+        final = last and c == C - 1
+        p0 = lambda: P.matmul(acc_, T.xsel[:, 0:128], came if t else T.raw[:, a:b], t == 0, False)
+        if t == 0:
+            op(("p0", c), "P", ["carry", ("xsel", 0)], p0)
+
         def pa():
-            if last:
-                P.matmul(acc_, T.idf[:, :], T.plf[:, a:b], True, False)
             for s in range(S - 1, 1, -1):
-                r = P.matmul(acc_, T.xsel[:, s * 128:(s + 1) * 128], slot(T.xb, s - 1), s == S - 1 and not last, False)
+                r = P.matmul(acc_, T.xsel[:, s * 128:(s + 1) * 128], slot(T.xb, s - 1), t > 0 and s == S - 1, False)
+            if final:
+                r = P.matmul(acc_, T.idf[:, :], T.plk[:, a:b], False, False)
             return r
-        op(("pa", c, t), "P", gathers + [("xsel", S - 1), "idf"]
-           + back("conv" if m - 3 >= (RO - 1) * C else "add", 3), pa)
+        op(("pa", c, t), "P", gathers + [("xsel", S - 1), "idf"] + ([("lack", C - 1, t - 1)] if final else []), pa)
 
         def px():
-            P.matmul(acc_, T.xsel[:, 0:128], came, False, False)
+            if t:
+                p0()
             return P.matmul(acc_, T.xsel[:, 128:256], slot(T.xb, 0), False, False)
         op(("px", c, t), "P", [("ins", c, t)], px)
         op(("pc", c, t), "P", [("scan", c, t)], lambda: P.matmul(pc_, move, slot(T.qb, S - 1), False, True))
@@ -181,53 +221,79 @@ def rank_program(g, core, T, topo):
                 r = P.matmul(acc_, T.qw[:, S - k:S - k + 128], slot(T.qb, k - 1), False, k == S - 1)
             return r
         op(("pq", c, t), "P", [("scan", c, t), "qw"], pq)
-        op(("q16", c, t), "V", [("pc", c, t)] + ([("ev", c, t - 1)] if t else []),
-           lambda: V.tensor_scalar(T.q16[:, a:b], pc_, -7.5 if last else -16.0, None, A.add))
-        op(("ev", c, t), "V", [("q16", c, t)], lambda: V.tensor_tensor(made, pc_, T.q16[:, a:b], A.subtract))
+        whole, less = T.pb[:, t * J + a:t * J + b], T.nq[:, t * J + a:t * J + b]
+        if last:
+            op(("q16", c, t), "V", [("pc", c, t)], lambda: V.tensor_scalar(less, pc_, -7.5, None, A.add))
+            op(("ev", c, t), "V", [("q16", c, t)], lambda: V.tensor_tensor(made, pc_, less, A.subtract))
+        else:
+            op(("q16", c, t), "V", [("pc", c, t)], lambda: V.tensor_scalar(less, pc_, BF, -(BF - 16), A.add, A.add))
+            op(("ev", c, t), "V", [("pc", c, t)], lambda: V.tensor_scalar(whole, pc_, -1.0, -8.0, A.mult, A.add))
+        if not final:
+            op(("add", c, t), "V", [("pq", c, t), ("lack", C - 1, t - 1) if t else "plk"],
+               lambda: V.tensor_tensor((T.plf if last else T.off)[:, a:b], (T.plk if last else T.ofk)[:, a:b], acc_, A.add))
         if not last:
-            op(("add", c, t), "V", [("pq", c, t), "plf"],
-               lambda: V.tensor_tensor(T.plf[:, a:b], T.plf[:, a:b], acc_, A.add))
-            op(("conv", c, t), "V", [("add", c, t), "kc"],
-               lambda: V.tensor_scalar(T.off[:, a:b], T.plf[:, a:b], T.kc[:, t:t + 1], None, A.add))
             if c == C - 1:
-                op(("fix", c, t), "S", [("ev", c, t)],
-                   lambda: Sc.activation(T.ycb[:, t * J:(t + 1) * J], T.cb[:, t * J:(t + 1) * J], F.Identity, bias=-8.5))
+                out, more = (T.plk, BW - PAD) if t == RO - 2 else (T.ofk, 0.0)
+                op(("lack", c, t), "V", [("add", e, t) for e in range(C)],
+                   lambda: V.tensor_scalar(out[:, :], T.off[:, :], T.col[:, 1:2], more - 8.0, A.add, A.add))
             dst = T.cores[(rank + 1 + t % (N - 1)) % N]
             src = T.cores[(rank - 1 - t % (N - 1)) % N]
-            rid, pid = topo.addr(dst)[0:2]
             name = "arr%d_%d" % (c, t)
-            op(("rem", c, t), "G", [("ev", c, t)],
-               lambda: g.remote_dma(T.land[:, (t + 1) * J + a:(t + 1) * J + b], made,
-                                    T.sem[name], T.sem.sent, pid, rid, topo.mask(core, dst)),
+            there = T.land[:, (t + 1) * J + a:(t + 1) * J + b]
+            op(("rem", c, t), "G", [("ev", c, t), ("q16", c, t)],
+               lambda: fold(dst, topo.mask(core, dst), name, "sent", [whole, less], there),
                "sent", len(topo.engines(core, dst)))
             op(("arr", c, t), None, [], None, name, len(topo.engines(src, core)))
+            for i, (t0, t1) in enumerate(VIA):
+                if c == C - 1 and t == t1 - 1:
+                    u, w = t0 * J, t1 * J
+                    op(("sum", c, t), "G", [(k, e, s) for k in ("ev", "q16") for e in range(C) for s in range(t0, t1)] + ["half"],
+                       lambda i=i, u=u, w=w: fold(aid, spare, "got%d" % i, "lent",
+                                                  [T.pb[:, u:w], T.nq[:, u:w], T.half[:, 0:w - u]], T.cb[:, u:w]),
+                       "lent", bin(spare).count("1"))
         else:
-            op(("add", c, t), "V", [("pq", c, t)],
-               lambda: V.tensor_scalar(T.msk[:, a:b], acc_, float(W), -float(W), A.is_ge, A.mult))
-            op(("conv", c, t), "V", [("add", c, t)],
-               lambda: V.tensor_tensor(T.ypo[:, a:b], acc_, T.msk[:, a:b], A.add))
-            if c >= C - 2:
-                lo = a if c == C - 1 else 0
-                op(("yp", c), "Y", [("conv", c, t)], lambda: Y.dma_start(T.yp[:, lo:b], T.ypo[:, lo:b]), "out", 16)
-                op(("ycl", c), "Y", [("ev", c, t)],
-                   lambda: Y.dma_start(T.yc[:, t * J + lo:t * J + b], T.cb[:, t * J + lo:t * J + b]), "out", 16)
+            have = acc_ if final else T.plf[:, a:b]
+            if final:
+                op(("rnd", c, t), "V", [("pq", c, t)], lambda: V.tensor_scalar(T.msk[:, a:b], have, 0.5 - W / 2, None, A.add))
+            else:
+                op(("rnd", c, t), "S", [("add", c, t)], lambda: Sc.activation(T.msk[:, a:b], have, F.Identity, bias=0.5 - W / 2))
+            op(("fin", c, t), "V", [("rnd", c, t)],
+               lambda: V.tensor_tensor(T.ypo[:, a:b], have, T.msk[:, a:b], A.subtract))
     for t in range(RO):
         for c in range(C):
             step(c, t)
 
-    done = [("fix", C - 1, RO - 2), ("rem", C - 1, RO - 2)]
-    op(("yc", 0), "Y", done, lambda: Y.dma_start(T.yc[0:112, 0:(RO - 1) * J], T.ycb[16:128, :]), "out", 16)
-    op(("yc", 1), "Y", done, lambda: Y.dma_start(T.yc[112:128, 0:(RO - 1) * J], T.ycb[0:16, :]), "out", 16)
+    op("back", None, [], None, "back", (len(VIA) - 1) * len(topo.engines(aid, core)))
+    op("late", None, [], None, "late", len(topo.engines(aid, core)))
+    for i, (wait, u, w) in enumerate((("back", 0, VIA[-1][0] * J), ("late", VIA[-1][0] * J, VIA[-1][1] * J))):
+        done = [("rem", c, RO - 2) for c in range(C)] + [wait]
+        op(("yc", i, 0), "Y", done, lambda u=u, w=w: Y.dma_start(T.yc[0:112, u:w], T.cb[16:128, u:w]), "out", 16)
+        op(("yc", i, 1), "Y", done, lambda u=u, w=w: Y.dma_start(T.yc[112:128, u:w], T.cb[0:16, u:w]), "out", 16)
     order = {
-        "G": ["pi", "ee", "uu", "base"] + periodic(PAT_G, ops),
-        "V": ["one", "cw0", "cw", "ci", "pm", "idf", "pmf", "idp", "dd", "cs1", "d1", "cs", "d2", "kc", "qw", "shp"]
-             + [("xsel", s) for s in range(S // 2)] + ["off0", "plf"] + [("xsel", s) for s in range(S // 2, S)]
-             + periodic(PAT_V, ops)[:1] + ["c85"] + periodic(PAT_V, ops)[1:],
-        "S": ["place", "ab"] + periodic(PAT_S, ops),
-        "P": periodic(PAT_P, ops),
-        "Y": ["ring", "carry"] + [("ext", i) for i in range(len(EXT))] + [("yc", 0), ("yc", 1)]
-             + [x for c in (C - 2, C - 1) for x in (("ycl", c), ("yp", c))],
+        "G": ["pi", "ee", "nil", "base"] + periodic(PAT_G, ops, "G"),
+        "V": ["pad", "one", "half", "cw0", "cw", "pm", "idf", "pmf", "idp", "dd", "cs", "c0", "d1", "qw", "d2", "shn"]
+             + [("xsel", s) for s in range(S // 2)] + ["off0", "plk"] + [("xsel", s) for s in range(S // 2, S)]
+             + periodic(PAT_V, ops, "V")[:1] + ["c85"] + periodic(PAT_V, ops, "V")[1:],
+        "S": ["place", "carry", "ab"] + periodic(PAT_S, ops, "S"),
+        "P": [("p0", c) for c in range(C)] + periodic(PAT_P, ops, "P"),
     }
+    order["P"] = order["P"][:C] + HEAD_P + [x for x in order["P"][C:] if x not in HEAD_P]
+    order["V"] = [x for x in order["V"] if x not in TAIL_V] + TAIL_V
+    E = RO - 1
+    end = order["V"][-1][1]
+    for i, (lo, hi) in enumerate(((0, end), (end + 1, C), (end, end + 1))):
+        if lo < hi:
+            a, b = LO[lo], LO[hi - 1] + NS[hi - 1]
+            op(("yp", i), "Y", [("fin", c, E) for c in range(lo, hi)],
+               lambda a=a, b=b: Y.dma_start(T.yp[:, a:b], T.ypo[:, a:b]), "out", 16)
+            op(("ycl", i), "Y", [("ev", c, E) for c in range(lo, hi)],
+               lambda a=a, b=b: Y.dma_start(T.yc[:, E * J + a:E * J + b], T.cb[:, E * J + a:E * J + b]), "out", 16)
+    order["Y"] = (["ring"] + [("ext", i) for i in range(len(EXT))] + [("yc", i, j) for i in range(2) for j in range(2)]
+                  + [(k, i) for i in range(3) for k in ("ycl", "yp") if (k, i) in ops])
+    assert sorted(map(str, sum(order.values(), []))) == sorted(str(x) for x in ops if ops[x][0])
+    for t in range(RO):
+        for c in range(C):
+            assert order["P"].index(("pa", c, t)) < order["P"].index(("px", c, t)) < order["P"].index(("pq", c, t))
 
     total, at = {}, {}
     for q in order:
@@ -271,7 +337,7 @@ def rank_program(g, core, T, topo):
             for sem, val in waits:
                 queue[q].wait_ge(T.sem[sem], val)
             r = ops[name][2]()
-            if ops[name][3] != "sent":
+            if ops[name][3] not in ("sent", "lent"):
                 r.then_inc(T.sem[ops[name][3]], ops[name][4])
     for sem in total:
         if waited.get(sem, 0) < total[sem]:

from concourse.bass import DstId, RemoteDMATransfer
from concourse.mybir import AluOpType as A, ActivationFunctionType as F

W, S, J, RO = 4096, 16, 256, 12
GROW = 15 * 16
B = 3072.0
BW = 1.5 * 128 * W
BF = 1.5 * 2 ** 27
PAD = 16
VIA = [(t, min(t + 2, RO - 1)) for t in range(0, RO - 1, 2)]
NS = [64, 64, 64, 64]
VS = [16, 16, 14, 16]
V0 = [32, 30, 16, 16]
VL = [14, 16, 14, 14]
C = len(NS)
NM = max(NS)
LO = [sum(NS[:c]) for c in range(C)]
EXT = [(1, 2), (3, 11)]
PAT_V = [("scan", 0), ("add", -1), ("fin", -2), ("gV", 2), ("z", 1), ("lack", -1), ("rnd", -1), ("ins", 1), ("q16", 0), ("ev", 0)]
HEAD_P = [("p15", 0, 0), ("pa", 0, 0), ("p15", 1, 0), ("pa", 1, 0)]
TAIL_V = [("scan", 3, 11), ("add", 2, 11), ("fin", 1, 11), ("q16", 3, 11), ("fin", 2, 11), ("ev", 3, 11), ("rnd", 3, 11), ("fin", 3, 11)]
PAT_S = [("gS", 3), ("rnd", -1)]
PAT_P = [("p15", 1), ("pc", 0), ("px", 0), ("pq", 0), ("pa", 1)]
PAT_G = [("rem", -1), ("z", 1), ("sum", -1)]

SCRATCH = {
    "win": ("sbuf", [128, PAD + W + GROW * (RO - 1)], "bfloat16"),
    "xb": ("sbuf", [128, J * S], "bfloat16"),
    "qb": ("sbuf", [128, J * S], "bfloat16"),
    "nil": ("sbuf", [128, NM * S], "bfloat16"),
    "base": ("sbuf", [128, NM * S], "float16"),
    "land": ("sbuf", [128, RO * J], "bfloat16"),
    "cb": ("sbuf", [128, RO * J], "bfloat16"),
    "pb": ("sbuf", [128, RO * J], "bfloat16"),
    "nq": ("sbuf", [128, RO * J], "bfloat16"),
    "off": ("sbuf", [128, J], "uint16"),
    "plc": ("sbuf", [128, J], "int32"),
    "plf": ("sbuf", [128, J], "float32"),
    "msk": ("sbuf", [128, J], "bfloat16"),
    "ypo": ("sbuf", [128, J], "float32"),
    "pi": ("sbuf", [128, 8], "int32"),
    "col": ("sbuf", [128, 8], "float32"),
    "raw": ("sbuf", [128, J], "bfloat16"),
    "ofk": ("sbuf", [128, J], "uint16"),
    "plk": ("sbuf", [128, J], "float32"),
    "ee": ("sbuf", [128, 144], "bfloat16"),
    "dd": ("sbuf", [128, 144], "bfloat16"),
    "d1": ("sbuf", [128, 128], "bfloat16"),
    "d2": ("sbuf", [128, 128], "bfloat16"),
    "ab": ("sbuf", [128, 128], "bfloat16"),
    "half": ("sbuf", [128, 2 * J], "bfloat16"),
    "qw": ("sbuf", [128, 144], "bfloat16"),
    "xsel": ("sbuf", [128, S * 128], "bfloat16"),
    "shn": ("sbuf", [128, 128], "bfloat16"),
    "idp": ("sbuf", [128, 128], "bfloat16"),
    "idf": ("sbuf", [128, 128], "float32"),
    "one": ("sbuf", [128, NM], "bfloat16"),
    "cw": ("sbuf", [128, 128], "bfloat16"),
}
for _c in range(C):
    SCRATCH["pc%d" % _c] = ("psum", [128, 512], "float32")
    SCRATCH["acc%d" % _c] = ("psum", [128, 512], "float32")

SEMAPHORES = (["cV", "cS", "cP", "cG", "ring", "place", "carry", "sent", "out", "lent", "back", "late"]
              + ["got%d" % i for i in range(len(VIA))]
              + ["ext%d" % i for i in range(len(EXT))]
              + ["arr%d_%d" % (c, t) for c in range(C) for t in range(RO - 1)])


def periodic(pat, ops, q):
    seq = []
    for m in range(-2 * C, (RO + 2) * C):
        for k, d in pat:
            name = (k, (m + d) % C, (m + d) // C)
            if name in ops and ops[name][0] == q:
                seq.append(name)
    return seq


def helper_of(core, cores, topo):
    return [c for c in topo.cores_of(core) if c not in cores and topo.die(c) == topo.die(core)][0]


def hand_back(g, core, owner, T, topo):
    rid, pid = topo.addr(owner)[0:2]
    off_chip = topo.mask(owner, [c for c in T.cores if c != owner][0])
    for i, (u, w) in enumerate(VIA):
        g.wait_ge(T.sem["got%d" % i], bin(topo.mask(owner, core) & ~off_chip).count("1"))
        piece = T.cb[:, u * J:w * J]
        g.remote_dma(piece, piece, T.sem["late" if w == RO - 1 else "back"], T.sem.lent, pid, rid, topo.mask(core, owner))
    g.wait_ge(T.sem.lent, len(VIA) * len(topo.engines(core, owner)))


def rank_program(g, core, T, topo):
    rank = T.rank_of(core)
    if rank is None:
        for owner in T.cores:
            if helper_of(owner, T.cores, topo) == core:
                hand_back(g, core, owner, T, topo)
        return
    N = len(T.cores)
    aid = helper_of(core, T.cores, topo)
    spare = topo.mask(core, aid) & ~topo.mask(core, T.cores[(rank + 1) % N])

    def fold(dst, mask, there, here, srcs, out):
        rid, pid = topo.addr(dst)[0:2]
        return g.remote_dma_fused([RemoteDMATransfer(
            dst_ids=[DstId(rid=rid, pnc=pid)], dma_engine_mask=mask, remote_sem=T.sem[there],
            srcs=srcs, dsts=[out], alu_op=1)], local_sem=T.sem[here])
    V, Sc, P, Y = g.vector, g.scalar, g.tensor, g.sync
    queue = {"V": V, "S": Sc, "P": P, "G": g, "Y": Y}
    ops = {}

    def op(name, q, deps, fn, sem=None, inc=1):
        ops[name] = (q, list(deps), fn, sem or "c" + q, inc)

    small = dict(allow_small_or_imprecise_dtypes=True)

    op("ring", "Y", [], lambda: Y.dma_start(T.win[:, PAD:PAD + W], T.ring[:, :]), "ring", 16)
    op("place", "S", [], lambda: Sc.dma_start(T.plc[:, :], T.place[:, :]), "place", 16)
    op("carry", "S", [], lambda: Sc.dma_start(T.raw[:, :], T.carry[:, :]), "carry", 16)

    def ext(i):
        a, b = GROW * (EXT[i][0] - 1), GROW * EXT[i][1]
        return lambda: Y.dma_start(T.win[:, PAD + W + a:PAD + W + b], T.ring[:, a:b])
    for i in range(len(EXT)):
        op(("ext", i), "Y", ["ring"], ext(i), "ext%d" % i, 16)

    op("pi", "G", [], lambda: g.iota(T.pi[:, 0:1], [[0, 1]], 0, 1))
    op("ee", "G", [], lambda: g.iota(T.ee[:, :], [[1, 144]], 0, -1, **small))
    op("nil", "G", [], lambda: g.iota(T.nil[:, :], [[0, NM * S]], 0, 0, **small))
    op("base", "G", ["nil"], lambda: g.affine_select(T.base[:, :], T.nil[:, :], [[0, NM * S]], A.is_gt, B + 8, 0, 0))
    op("one", "V", [], lambda: V.memset(T.one[:, :], 1.0))
    op("half", "V", [], lambda: V.memset(T.half[:, :], -0.5))
    op("cw0", "V", [], lambda: V.memset(T.cw[0:32, :], (B + 128) / 32))
    op("cw", "V", [], lambda: V.memset(T.cw[32:64, :], 7.5 / 32))
    op("c85", "V", ["carry"], lambda: V.tensor_scalar(T.land[:, 0:J], T.raw[:, :], 0.5, None, A.add))
    op("pm", "V", ["pi"], lambda: V.tensor_scalar(T.pi[:, 4:5], T.pi[:, 0:1], 15, None, A.bitwise_and))
    op("pmf", "V", ["pm"], lambda: V.tensor_copy(T.col[:, 0:1], T.pi[:, 4:5]))
    op("idf", "V", ["ee"], lambda: V.tensor_scalar(T.idf[:, :], T.ee[:, 0:128], 0.0, None, A.is_equal))
    op("idp", "V", ["ee"], lambda: V.tensor_scalar(T.idp[:, :], T.ee[:, 0:128], 0.0, None, A.is_equal))
    op("dd", "V", ["pmf", "ee"], lambda: V.tensor_scalar(T.dd[:, :], T.ee[:, :], T.col[:, 0:1], None, A.add))
    op("cs", "V", ["pmf"], lambda: V.tensor_scalar(T.col[:, 1:2], T.col[:, 0:1], 1.0, 16 * (B + 16), A.is_ge, A.mult))
    op("d1", "V", ["dd"], lambda: V.tensor_scalar(T.d1[:, :], T.dd[:, 0:128], 16.0, -128.0, A.is_ge, A.mult))
    op("d2", "V", ["d1"], lambda: V.tensor_tensor(T.d2[:, :], T.dd[:, 0:128], T.d1[:, :], A.add))
    op("qw", "V", ["dd"], lambda: V.tensor_scalar(T.qw[:, :], T.dd[:, :], 16.0, -1.0, A.is_equal, A.mult))

    def xsel(s):
        return lambda: V.tensor_scalar(T.xsel[:, s * 128:(s + 1) * 128], T.d2[:, :], float(s), None,
                                       A.is_ge if s else A.is_equal)
    for s in range(S):
        op(("xsel", s), "V", ["d2"], xsel(s))
    op("ab", "S", ["ee"], lambda: Sc.activation(T.ab[:, :], T.ee[:, 0:128], F.Abs, bias=48.0))
    op("shn", "V", ["ab"], lambda: V.tensor_scalar(T.shn[:, :], T.ab[:, :], 64.0, -1.0, A.is_equal, A.mult))
    op("pad", "V", [], lambda: V.memset(T.win[:, 0:PAD], 0.0))
    op("off0", "V", ["place", "pad"], lambda: V.tensor_scalar(T.off[:, :], T.plc[:, :], float(PAD), None, A.add))
    op("c0", "V", ["pmf"], lambda: V.tensor_scalar(T.col[:, 2:3], T.col[:, 0:1], 1.0, 16 * (B + 16) - 8, A.is_ge, A.mult))
    op("plk", "V", ["place", "c0"], lambda: V.tensor_scalar(T.ofk[:, :], T.plc[:, :], T.col[:, 2:3], float(PAD), A.add, A.add))

    def step(c, t):
        n, a = NS[c], LO[c]
        b = a + n
        last = t == RO - 1
        v = (V0 if t == 0 else VL if last else VS)[c]
        pc_, acc_ = T["pc%d" % c][:, 0:n], T["acc%d" % c][:, 0:n]
        move = (T.idp if last else T.shn)[:, :]
        before = lambda k: [(k, c, t - 1)] if t else []
        slot = lambda buf, s: buf[:, a * S + s:b * S:S]
        came = T.land[:, t * J + a:t * J + b]
        made = T.cb[:, t * J + a:t * J + b]
        piece = [i for i in range(len(EXT)) if EXT[i][0] <= t <= EXT[i][1]]
        wide = PAD + W + (GROW * EXT[piece[0]][1] if piece else 0)
        pre = ["ring", "off0"] if t == 0 else [("add", c, t - 1), ("ext", piece[0])]
        gathers = []
        if v < n:
            op(("gS", c, t), "S", pre,
               lambda: Sc.activation(T.xb[:, (a + v) * S:b * S], T.win[:, 0:wide].indirect(T.off[:, a + v:b]), F.Copy))
            gathers.append(("gS", c, t))
        if v:
            op(("gV", c, t), "V", pre,
               lambda: V.tensor_copy(T.xb[:, a * S:(a + v) * S], T.win[:, 0:wide].indirect(T.off[:, a:a + v])))
            gathers.append(("gV", c, t))

        def p15():
            if last:
                P.matmul(pc_, T.cw[0:64, :], T.one[0:64, 0:n], True, False)
            return P.matmul(pc_, move, slot(T.xb, S - 1), not last, False)
        op(("p15", c, t), "P", gathers + before("ev") + before("q16") + ["cw", "one", "idp", "shn"], p15)
        if (c, t) == (2, 0):
            op(("z", c, t), "V", [("p15", c, t)], lambda: V.memset(slot(T.xb, S - 1), -B - 128))
        else:
            op(("z", c, t), "G", [("p15", c, t)], lambda: g.iota(slot(T.xb, S - 1), [[0, n]], -int(B) - 128, 0, **small))

        op(("ins", c, t), "V", gathers + [("arr", c, t - 1) if t else "c85"],
           lambda: V.tensor_tensor(slot(T.xb, 0), slot(T.xb, 0), came, A.add))
        op(("scan", c, t), "V", [("ins", c, t), ("z", c, t), "base"] + before("pq"),
           lambda: V.tensor_tensor_scan(T.qb[:, a * S:b * S], T.base[:, 0:n * S], T.xb[:, a * S:b * S], 0.0, A.max, A.add))

        final = last and c == C - 1
        p0 = lambda: P.matmul(acc_, T.xsel[:, 0:128], came if t else T.raw[:, a:b], t == 0, False)
        if t == 0:
            op(("p0", c), "P", ["carry", ("xsel", 0)], p0)

        def pa():
            for s in range(S - 1, 1, -1):
                r = P.matmul(acc_, T.xsel[:, s * 128:(s + 1) * 128], slot(T.xb, s - 1), t > 0 and s == S - 1, False)
            if final:
                r = P.matmul(acc_, T.idf[:, :], T.plk[:, a:b], False, False)
            return r
        op(("pa", c, t), "P", gathers + [("xsel", S - 1), "idf"] + ([("lack", C - 1, t - 1)] if final else []), pa)

        def px():
            if t:
                p0()
            return P.matmul(acc_, T.xsel[:, 128:256], slot(T.xb, 0), False, False)
        op(("px", c, t), "P", [("ins", c, t)], px)
        op(("pc", c, t), "P", [("scan", c, t)], lambda: P.matmul(pc_, move, slot(T.qb, S - 1), False, True))

        def pq():
            for k in range(1, S):
                r = P.matmul(acc_, T.qw[:, S - k:S - k + 128], slot(T.qb, k - 1), False, k == S - 1)
            return r
        op(("pq", c, t), "P", [("scan", c, t), "qw"], pq)
        whole, less = T.pb[:, t * J + a:t * J + b], T.nq[:, t * J + a:t * J + b]
        if last:
            op(("q16", c, t), "V", [("pc", c, t)], lambda: V.tensor_scalar(less, pc_, -7.5, None, A.add))
            op(("ev", c, t), "V", [("q16", c, t)], lambda: V.tensor_tensor(made, pc_, less, A.subtract))
        else:
            op(("q16", c, t), "V", [("pc", c, t)], lambda: V.tensor_scalar(less, pc_, BF, -(BF - 16), A.add, A.add))
            op(("ev", c, t), "V", [("pc", c, t)], lambda: V.tensor_scalar(whole, pc_, -1.0, -8.0, A.mult, A.add))
        if not final:
            op(("add", c, t), "V", [("pq", c, t), ("lack", C - 1, t - 1) if t else "plk"],
               lambda: V.tensor_tensor((T.plf if last else T.off)[:, a:b], (T.plk if last else T.ofk)[:, a:b], acc_, A.add))
        if not last:
            if c == C - 1:
                out, more = (T.plk, BW - PAD) if t == RO - 2 else (T.ofk, 0.0)
                op(("lack", c, t), "V", [("add", e, t) for e in range(C)],
                   lambda: V.tensor_scalar(out[:, :], T.off[:, :], T.col[:, 1:2], more - 8.0, A.add, A.add))
            dst = T.cores[(rank + 1 + t % (N - 1)) % N]
            src = T.cores[(rank - 1 - t % (N - 1)) % N]
            name = "arr%d_%d" % (c, t)
            there = T.land[:, (t + 1) * J + a:(t + 1) * J + b]
            op(("rem", c, t), "G", [("ev", c, t), ("q16", c, t)],
               lambda: fold(dst, topo.mask(core, dst), name, "sent", [whole, less], there),
               "sent", len(topo.engines(core, dst)))
            op(("arr", c, t), None, [], None, name, len(topo.engines(src, core)))
            for i, (t0, t1) in enumerate(VIA):
                if c == C - 1 and t == t1 - 1:
                    u, w = t0 * J, t1 * J
                    op(("sum", c, t), "G", [(k, e, s) for k in ("ev", "q16") for e in range(C) for s in range(t0, t1)] + ["half"],
                       lambda i=i, u=u, w=w: fold(aid, spare, "got%d" % i, "lent",
                                                  [T.pb[:, u:w], T.nq[:, u:w], T.half[:, 0:w - u]], T.cb[:, u:w]),
                       "lent", bin(spare).count("1"))
        else:
            have = acc_ if final else T.plf[:, a:b]
            if final:
                op(("rnd", c, t), "V", [("pq", c, t)], lambda: V.tensor_scalar(T.msk[:, a:b], have, 0.5 - W / 2, None, A.add))
            else:
                op(("rnd", c, t), "S", [("add", c, t)], lambda: Sc.activation(T.msk[:, a:b], have, F.Identity, bias=0.5 - W / 2))
            op(("fin", c, t), "V", [("rnd", c, t)],
               lambda: V.tensor_tensor(T.ypo[:, a:b], have, T.msk[:, a:b], A.subtract))
    for t in range(RO):
        for c in range(C):
            step(c, t)

    op("back", None, [], None, "back", (len(VIA) - 1) * len(topo.engines(aid, core)))
    op("late", None, [], None, "late", len(topo.engines(aid, core)))
    for i, (wait, u, w) in enumerate((("back", 0, VIA[-1][0] * J), ("late", VIA[-1][0] * J, VIA[-1][1] * J))):
        done = [("rem", c, RO - 2) for c in range(C)] + [wait]
        op(("yc", i, 0), "Y", done, lambda u=u, w=w: Y.dma_start(T.yc[0:112, u:w], T.cb[16:128, u:w]), "out", 16)
        op(("yc", i, 1), "Y", done, lambda u=u, w=w: Y.dma_start(T.yc[112:128, u:w], T.cb[0:16, u:w]), "out", 16)
    order = {
        "G": ["pi", "ee", "nil", "base"] + periodic(PAT_G, ops, "G"),
        "V": ["pad", "one", "half", "cw0", "cw", "pm", "idf", "pmf", "idp", "dd", "cs", "c0", "d1", "qw", "d2", "shn"]
             + [("xsel", s) for s in range(S // 2)] + ["off0", "plk"] + [("xsel", s) for s in range(S // 2, S)]
             + periodic(PAT_V, ops, "V")[:1] + ["c85"] + periodic(PAT_V, ops, "V")[1:],
        "S": ["place", "carry", "ab"] + periodic(PAT_S, ops, "S"),
        "P": [("p0", c) for c in range(C)] + periodic(PAT_P, ops, "P"),
    }
    order["P"] = order["P"][:C] + HEAD_P + [x for x in order["P"][C:] if x not in HEAD_P]
    order["V"] = [x for x in order["V"] if x not in TAIL_V] + TAIL_V
    E = RO - 1
    end = order["V"][-1][1]
    for i, (lo, hi) in enumerate(((0, end), (end + 1, C), (end, end + 1))):
        if lo < hi:
            a, b = LO[lo], LO[hi - 1] + NS[hi - 1]
            op(("yp", i), "Y", [("fin", c, E) for c in range(lo, hi)],
               lambda a=a, b=b: Y.dma_start(T.yp[:, a:b], T.ypo[:, a:b]), "out", 16)
            op(("ycl", i), "Y", [("ev", c, E) for c in range(lo, hi)],
               lambda a=a, b=b: Y.dma_start(T.yc[:, E * J + a:E * J + b], T.cb[:, E * J + a:E * J + b]), "out", 16)
    order["Y"] = (["ring"] + [("ext", i) for i in range(len(EXT))] + [("yc", i, j) for i in range(2) for j in range(2)]
                  + [(k, i) for i in range(3) for k in ("ycl", "yp") if (k, i) in ops])
    assert sorted(map(str, sum(order.values(), []))) == sorted(str(x) for x in ops if ops[x][0])
    for t in range(RO):
        for c in range(C):
            assert order["P"].index(("pa", c, t)) < order["P"].index(("px", c, t)) < order["P"].index(("pq", c, t))

    total, at = {}, {}
    for q in order:
        for name in order[q]:
            sem, inc = ops[name][3], ops[name][4]
            total[sem] = total.get(sem, 0) + inc
            at[name] = total[sem]
    known = {q: {} for q in order}
    clock = {}
    for name in ops:
        if ops[name][0] is None:
            at[name] = total[ops[name][3]] = ops[name][4]
            clock[name] = {ops[name][3]: at[name]}
    waited = {}
    calls = {q: [] for q in order}
    pos = {q: 0 for q in order}
    left = sum(len(x) for x in order.values())
    while left:
        before = left
        for q in order:
            while pos[q] < len(order[q]) and all(d in clock for d in ops[order[q][pos[q]]][1]):
                name = order[q][pos[q]]
                deps = ops[name][1]
                deps = [d for d in deps if not any(e != d and clock[e].get(ops[d][3], 0) >= at[d] for e in deps)]
                waits = []
                for d in deps:
                    sem = ops[d][3]
                    if known[q].get(sem, 0) < at[d]:
                        waits.append((sem, at[d]))
                        waited[sem] = max(waited.get(sem, 0), at[d])
                        for k, val in clock[d].items():
                            known[q][k] = max(known[q].get(k, 0), val)
                clock[name] = dict(known[q])
                clock[name][ops[name][3]] = at[name]
                calls[q].append((waits, name))
                pos[q] += 1
                left -= 1
        assert left < before, "the queues' orders wait for one another"
    for q in order:
        for waits, name in calls[q]:
            for sem, val in waits:
                queue[q].wait_ge(T.sem[sem], val)
            r = ops[name][2]()
            if ops[name][3] not in ("sent", "lent"):
                r.then_inc(T.sem[ops[name][3]], ops[name][4])
    for sem in total:
        if waited.get(sem, 0) < total[sem]:
            (Y if sem == "out" else g).wait_ge(T.sem[sem], total[sem])
